import numpy as np
CORES = [32,40,48,56,64,72,80,88,96,104,112,120]
N = 12
TK = 256
NT = N * TK
EPS = 0.01
def setup_inputs(rng):
    x = (rng.standard_normal((N, 128, TK), dtype=np.float32) * (0.5 + np.arange(N, dtype=np.float32).reshape(N, 1, 1) / N) + rng.standard_normal((N, 128, 1), dtype=np.float32))
    return {"x": x, "dy": (rng.standard_normal((N, 128, TK), dtype=np.float32) + 0.5 * x + rng.standard_normal((1, 128, 1), dtype=np.float32))}
def reference(x, dy):
    X = x.astype(np.float64)
    mu = X.sum(axis=(0, 2)).reshape(1, 128, 1) / NT
    rs = 1.0 / np.sqrt(((X - mu) ** 2).sum(axis=(0, 2)).reshape(1, 128, 1) / NT + EPS)
    n = (X - mu) * rs
    DY = dy.astype(np.float64)
    a = DY.sum(axis=(0, 2)).reshape(1, 128, 1) / NT; c = (DY * n).sum(axis=(0, 2)).reshape(1, 128, 1) / NT
    return {"dx": (rs * (DY - a - n * c)).astype(np.float32)}

from concourse.bass import DstId, RemoteDMATransfer
from concourse.mybir import AluOpType, AxisListType, ActivationFunctionType

N = 12
TK = 256
NT = N * TK
EPS = 0.01
E1 = 8
E2 = 4
CA = 96

_BIG = ("sbuf", [128, TK], "float32")
_COL = ("sbuf", [128, 1], "float32")
_BANK = ("psum", [128, 512], "float32")
SCRATCH = {
    "xs": _BIG, "dys": _BIG, "sqj": _BIG, "prod": _BIG, "xr": _BIG, "tt": _BIG, "zz": _BIG, "dxs": _BIG,
    "stx": ("sbuf", [128, 2], "float32"), "sty": ("sbuf", [128, 2], "float32"),
    "sel": ("sbuf", [128, 2], "float32"),
    "lx": ("sbuf", [128, TK + 4], "float32"), "ly": ("sbuf", [128, TK + 4], "float32"),
    "nv": _COL, "vv": _COL, "r2": _COL, "sd": _COL, "rs": _COL, "ww": _COL,
    "hx": ("dram", [128, 2], "float32"), "hy": ("dram", [128, 2], "float32"),
    "landx": ("dram", [N, 128, 2], "float32"), "landy": ("dram", [N, 128, 2], "float32"),
    "xp": _BANK, "dyp": _BANK, "psx": _BANK, "psy": _BANK,
}
SEMAPHORES = ["ldx", "ldy", "cst", "sx", "sy", "xpc", "prd", "sent", "hxa", "hya", "ax", "ay", "gx", "gy", "mx", "my",
              "nvs", "vs", "r2s", "xrs", "sq", "rss", "ws", "ts", "za", "zb", "fin", "st"]


def _engines(mask, n):
    bits = [b for b in range(mask.bit_length()) if (mask >> b) & 1]
    step = len(bits) // n
    return [bits[i * step] for i in range(n)]


def _helper(rank_core, T, topo):
    cand = [c for c in range(topo.CHIPS * topo.CORES_PER_CHIP)
            if c != rank_core and topo.chip(c) == topo.chip(rank_core)
            and all(topo.may_write(c, d) for d in T.cores)]
    cand.sort(key=lambda c: (topo.die(c) != topo.die(rank_core), c))
    return cand[0]


def _helper_program(g, core, rank, T, topo):
    S = T.sem
    common = topo.mask(core, T.cores[0])
    for d in T.cores:
        common &= topo.mask(core, d)
    eng = _engines(common, E2)

    def fan_out(src, land, sem):
        trs = []
        for i in range(E2):
            dsts = T.cores[i::E2]
            ids = []
            for d in dsts:
                rid, pid, _se = topo.addr(d)
                ids.append(DstId(rid=rid, pnc=pid))
            trs.append(RemoteDMATransfer(dst_ids=ids, dma_engine_mask=1 << eng[i], remote_sem=sem,
                                         srcs=[src[:]], dsts=[land[rank] for _d in dsts], alu_op=0))
        g.remote_dma_fused(trs, local_sem=S.sent)

    g.wait_ge(S.hxa, E1)
    fan_out(T.hx, T.landx, S.ax)
    g.wait_ge(S.hya, E1)
    fan_out(T.hy, T.landy, S.ay)
    g.wait_ge(S.sent, 2 * E2)


def _rank_program(g, core, T, topo):
    S = T.sem
    A = AluOpType
    F = ActivationFunctionType
    X = AxisListType.X
    v, s, pe, sy = g.vector, g.scalar, g.tensor, g.sync
    helper = _helper(core, T, topo)
    rid, pid, _se = topo.addr(helper)
    m1 = 0
    for b in _engines(topo.mask(core, helper), E1):
        m1 |= 1 << b

    sy.dma_start(T.xs[:], T.x[:]).then_inc(S.ldx, 16)
    s.dma_start(T.dys[:], T.dy[:]).then_inc(S.ldy, 16)

    g.wait_ge(S.sx, 2)
    g.remote_dma(out_ap=T.hx[:], in_ap=T.stx[:], remote_sem=S.hxa, local_sem=S.sent, pid=pid, routing_id=rid,
                 dma_engine_mask=m1)
    g.wait_ge(S.sy, 2)
    g.remote_dma(out_ap=T.hy[:], in_ap=T.sty[:], remote_sem=S.hya, local_sem=S.sent, pid=pid, routing_id=rid,
                 dma_engine_mask=m1)
    g.wait_ge(S.sent, 2 * E1)

    sy.wait_ge(S.ax, N)
    sy.dma_start(T.lx[0:N, 0:TK], T.landx[:]).then_inc(S.gx, 16)
    sy.wait_ge(S.ay, N)
    sy.dma_start(T.ly[0:N, 0:TK], T.landy[:]).then_inc(S.gy, 16)
    sy.dma_start(T.ly[N:2 * N, 1:TK + 1], T.landy[:]).then_inc(S.gy, 16)
    sy.wait_ge(S.fin, 2)
    sy.dma_start(T.dx[:], T.dxs[:]).then_inc(S.st, 16)
    sy.wait_ge(S.st, 16)

    pe.wait_ge(S.cst, 4)
    pe.wait_ge(S.gx, 32)
    pe.matmul(T.psx[:, 0:2], T.lx[0:2 * N, 1:TK:2], T.sel[0:2 * N, :], True, True).then_inc(S.mx, 1)
    pe.wait_ge(S.gy, 32)
    pe.matmul(T.psy[:, 0:2], T.ly[0:2 * N, 1:TK:2], T.sel[0:2 * N, :], True, True).then_inc(S.my, 1)

    s.wait_ge(S.ldx, 16)
    s.activation(T.sqj[:], T.xs[:], F.Square, accum_out=T.stx[:, 1:2]).then_inc(S.sx, 1)
    s.activation(T.xp[:, 0:TK], T.xs[:], F.Copy).then_inc(S.xpc, 1)
    s.wait_ge(S.ldy, 16)
    s.activation(T.dyp[:, 0:TK], T.dys[:], F.Copy, accum_out=T.sty[:, 0:1]).then_inc(S.sy, 1)
    s.wait_ge(S.ax, N)
    s.dma_start(T.lx[N:2 * N, 1:TK + 1], T.landx[:]).then_inc(S.gx, 16)
    s.wait_ge(S.nvs, 1)
    s.activation(T.sd[:], T.nv[:], F.Sqrt, bias=EPS, scale=-1.0).then_inc(S.sq, 1)
    s.wait_ge(S.sq, 1)
    s.wait_ge(S.r2s, 1)
    s.activation(T.rs[:], T.sd[:], F.Identity, scale=T.r2[:]).then_inc(S.rss, 1)
    s.wait_ge(S.rss, 1)
    s.wait_ge(S.za, 1)
    s.activation(T.dxs[:, 0:CA], T.zz[:, 0:CA], F.Identity, scale=T.rs[:]).then_inc(S.fin, 1)

    v.memset(T.sel[0:2 * N, 0:1], 1.0 / NT).then_inc(S.cst, 1)
    v.memset(T.sel[0:2 * N, 1:2], 0.0).then_inc(S.cst, 1)
    v.wait_ge(S.cst, 2)
    v.memset(T.sel[0:N, 0:1], 0.0).then_inc(S.cst, 1)
    v.memset(T.sel[0:N, 1:2], 1.0 / NT).then_inc(S.cst, 1)
    v.wait_ge(S.ldx, 16)
    v.tensor_reduce(T.stx[:, 0:1], T.xs[:], X, A.add).then_inc(S.sx, 1)
    v.wait_ge(S.ldy, 16)
    v.wait_ge(S.xpc, 1)
    v.tensor_tensor(T.prod[:], T.xp[:, 0:TK], T.dys[:], A.mult).then_inc(S.prd, 1)
    v.wait_ge(S.prd, 1)
    v.tensor_reduce(T.sty[:, 1:2], T.prod[:], X, A.add).then_inc(S.sy, 1)
    mu, q = T.psx[:, 0:1], T.psx[:, 1:2]
    a, p = T.psy[:, 0:1], T.psy[:, 1:2]
    v.wait_ge(S.mx, 1)
    v.tensor_scalar(T.nv[:], mu, mu, q, A.mult, A.subtract).then_inc(S.nvs, 1)
    v.wait_ge(S.nvs, 1)
    v.tensor_scalar(T.vv[:], T.nv[:], -1.0, EPS, A.mult, A.add).then_inc(S.vs, 1)
    v.wait_ge(S.vs, 1)
    v.reciprocal(T.r2[:], T.vv[:]).then_inc(S.r2s, 1)
    v.wait_ge(S.r2s, 1)
    v.tensor_scalar(T.xr[:], T.xs[:], mu, T.r2[:], A.subtract, A.mult).then_inc(S.xrs, 1)
    v.wait_ge(S.my, 1)
    v.tensor_scalar(T.ww[:], a, mu, p, A.mult, A.subtract).then_inc(S.ws, 1)
    v.wait_ge(S.ws, 1)
    v.wait_ge(S.xrs, 1)
    v.tensor_scalar(T.tt[:], T.xr[:], T.ww[:], a, A.mult, A.subtract).then_inc(S.ts, 1)
    v.wait_ge(S.ts, 1)
    v.wait_ge(S.sy, 2)
    v.tensor_tensor(T.zz[:, 0:CA], T.tt[:, 0:CA], T.dyp[:, 0:CA], A.add).then_inc(S.za, 1)
    v.tensor_tensor(T.zz[:, CA:TK], T.tt[:, CA:TK], T.dyp[:, CA:TK], A.add).then_inc(S.zb, 1)
    v.wait_ge(S.zb, 1)
    v.wait_ge(S.sq, 1)
    v.tensor_scalar(T.dxs[:, CA:TK], T.zz[:, CA:TK], T.sd[:], T.r2[:], A.mult, A.mult).then_inc(S.fin, 1)


def rank_program(g, core, T, topo):
    if T.rank_of(core) is not None:
        _rank_program(g, core, T, topo)
        return
    for r, c in enumerate(T.cores):
        if topo.chip(c) == topo.chip(core) and _helper(c, T, topo) == core:
            _helper_program(g, core, r, T, topo)
            return
